import numpy as np
import ml_dtypes


def mxq(x, axis, fmt="e4m3"):
    dtype, down = {"e4m3": (ml_dtypes.float8_e4m3fn, 7), "e5m2": (ml_dtypes.float8_e5m2, 14)}[fmt]
    v = np.moveaxis(np.asarray(x, np.float32).astype(ml_dtypes.bfloat16).astype(np.float64), axis, -1)
    blocks = v.reshape(v.shape[:-1] + (-1, 32))
    amax = np.abs(blocks).max(-1, keepdims=True)
    byte = np.maximum(np.where(amax > 0, np.frexp(amax)[1] - 1 + 127, 0) - down, 1)
    scale = np.exp2(byte - 127.0)
    codes = (blocks / scale).astype(np.float32).astype(dtype).astype(np.float64)
    return np.moveaxis((codes * scale).reshape(v.shape), -1, axis)


WIDE = False


def mx_kscale(k):
    if not WIDE:
        return np.ones(k)
    levels = np.array([10, -10, 5, -5, 0])
    if k % 512:
        return np.exp2(np.random.permutation(np.resize(levels, k // 32))).repeat(32)
    a = np.empty((k // 512, 16))
    for p in range(k // 512):
        a[p, :8] = np.random.permutation(np.resize(levels, 8))
        for g in range(8):
            far = levels[np.abs(levels - a[p, g]) >= 10]
            a[p, g + 8] = far[np.random.randint(len(far))]
    return np.exp2(a.ravel()).repeat(32)


def f64(x):
    return np.asarray(x).astype(np.float64)


def striped(idx):
    return np.tile(idx.reshape(-1, 16).T, (8, 1)).astype(np.uint16)


def unstriped(offs):
    return offs[:16].T.reshape(-1).astype(np.int64)


def pack_weight(w):
    k, n = w.shape
    w = f64(np.asarray(w, np.float32).astype(ml_dtypes.bfloat16)).reshape(k // 32, 32, n)
    amax = np.abs(w).max(1)
    byte = np.clip(np.where(amax > 0, np.frexp(amax)[1] - 1 + 127 - 7, 1), 1, 254)
    scaled = (w * np.exp2(127.0 - byte)[:, None, :]).reshape(k, n).astype(np.float32)
    words = np.ascontiguousarray(scaled.reshape(k // 512, 128, 4, n).transpose(0, 1, 3, 2)).astype(ml_dtypes.float8_e4m3fn).view(np.uint8)
    return words, np.ascontiguousarray(byte.astype(np.uint8).reshape(k // 512, 16, n))


def unpack_weight(words, scales):
    g, p, n, _ = words.shape
    vals = np.ascontiguousarray(words).view(ml_dtypes.float8_e4m3fn).astype(np.float64) * np.repeat(np.exp2(scales.astype(np.float64) - 127.0), 8, axis=1)[..., None]
    return vals.transpose(0, 1, 3, 2).reshape(g * 512, n)


E2M1 = np.array([0.0, 0.5, 1.0, 1.5, 2.0, 3.0, 4.0, 6.0, -0.0, -0.5, -1.0, -1.5, -2.0, -3.0, -4.0, -6.0])


def pack_fp4(w):
    k, n = w.shape
    w = f64(np.asarray(w, np.float32).astype(ml_dtypes.bfloat16)).reshape(k // 32, 32, n)
    amax = np.abs(w).max(1)
    mant, ex = np.frexp(amax / 6.0)
    byte = np.clip(np.where(amax > 0, np.where(mant > 0.5, ex, ex - 1) + 127, 1), 1, 254)
    scaled = (w * np.exp2(127.0 - byte)[:, None, :]).reshape(k, n).astype(np.float32)
    c = np.ascontiguousarray(scaled.reshape(k // 512, 128, 4, n).transpose(0, 1, 3, 2)).astype(ml_dtypes.float4_e2m1fn).view(np.uint8) & 0xF
    words = (c[..., 0::2] | (c[..., 1::2] << 4)).reshape(k // 512, 128, 2 * n)
    return np.ascontiguousarray(words), np.ascontiguousarray(byte.astype(np.uint8).reshape(k // 512, 16, n))


def unpack_fp4(words, scales):
    g, _, n = scales.shape
    words = np.ascontiguousarray(words).reshape(g, 128, n, 2)
    nib = np.empty((g, 128, n, 4), np.uint8)
    nib[..., 0::2] = words & 0xF
    nib[..., 1::2] = words >> 4
    vals = E2M1[nib] * np.repeat(np.exp2(scales.astype(np.float64) - 127.0), 8, axis=1)[..., None]
    return vals.transpose(0, 1, 3, 2).reshape(g * 512, n)


def planes(y):
    n, m = y.shape
    v = y.astype(np.float32).astype(ml_dtypes.bfloat16).astype(np.float64).reshape(n // 32, 32, m)
    top = np.abs(v).max(1)
    byte = np.clip(np.where(top > 0, np.frexp(top)[1] - 1 + 127 - 7, 1), 1, 254)
    codes = (v * np.exp2(127.0 - byte)[:, None, :]).reshape(n, m).astype(np.float32).astype(ml_dtypes.float8_e4m3fn).view(np.uint8)
    words = codes.reshape(n // 512, 128, 4, m).transpose(0, 1, 3, 2)
    return np.ascontiguousarray(words), np.ascontiguousarray(byte.astype(np.uint8).reshape(n // 512, 16, m))


K, T, S, N, H, U = 512, 2048, 512, 512, 512, 1024


def setup_inputs():
    n = np.random.standard_normal
    s = mx_kscale(K)[:, None]
    u = mx_kscale(H)
    packed_xT = pack_weight(n((K, T)) * s)
    packed_w1 = pack_fp4(n((K, N)) / np.sqrt(K) / s)
    packed_w2 = pack_fp4(n((K, N)) / np.sqrt(K) / s)
    packed_w3 = pack_fp4(n((H, N)) / np.sqrt(H) / u[:, None])
    return {
        "x_words": packed_xT[0],
        "x_scales": packed_xT[1],
        "w1_words": packed_w1[0],
        "w1_scales": packed_w1[1],
        "w2_words": packed_w2[0],
        "w2_scales": packed_w2[1],
        "unit": (np.random.uniform(0.6, 1.4, (H, 1)) * u[:, None]).astype(np.float32),
        "w3_words": packed_w3[0],
        "w3_scales": packed_w3[1],
        "offs": striped(np.random.permutation(T)[:S]),
        "s1": striped(np.random.permutation(np.concatenate([np.arange(S), np.random.randint(0, S, U - S)]))),
        "s2": striped(np.random.permutation(np.concatenate([np.arange(S), np.random.randint(0, S, U - S)]))),
    }


def reference(x_words, x_scales, w1_words, w1_scales, w2_words, w2_scales, unit, w3_words, w3_scales, offs, s1, s2):
    xq = unpack_weight(x_words, x_scales)[:, unstriped(offs)]
    y = unpack_fp4(w1_words, w1_scales).T @ xq
    y_1 = y[:, unstriped(s1)]
    z1 = unpack_fp4(w2_words, w2_scales).T @ xq
    z_2 = z1[:, unstriped(s2)]
    y_2 = y[:, unstriped(s2)]
    z_1 = z1[:, unstriped(s1)]
    dsg = y_2 - z_1
    hid = f64(unit) * ((y_1 * z_2) / (np.abs(dsg) + 0.8))
    out_0 = unpack_fp4(w3_words, w3_scales).T @ mxq(hid, 0, "e4m3")
    return (out_0,) + planes(out_0)

@@ -1,0 +1,231 @@
+from contextlib import ExitStack
+
+import concourse.mybir as mybir
+from concourse.masks import make_identity
+
+K, T, S, H, U = 512, 2048, 512, 512, 1024
+FLOPS = 2 * K * H * S * 2 + 2 * H * H * U
+
+F32 = mybir.dt.float32
+BF16 = mybir.dt.bfloat16
+I32 = mybir.dt.int32
+U32 = mybir.dt.uint32
+U16 = mybir.dt.uint16
+U8 = mybir.dt.uint8
+FP8X4 = mybir.dt.float8_e4m3fn_x4
+FP4X4 = mybir.dt.float4_e2m1fn_x4
+ACT = mybir.ActivationFunctionType
+ALU = mybir.AluOpType
+
+P = 128
+PACK = 4
+CHUNK = 256
+PAIR = 2
+
+
+def tile_picked_yfusgat_rel_po_kernel(
+    tc, x_words, x_scales, w1_words, w1_scales, w2_words, w2_scales, unit, w3_words, w3_scales, offs, s1, s2, out_0, out_1, out_2
+):
+    nc = tc.nc
+    with ExitStack() as ctx:
+        keep = ctx.enter_context(tc.tile_pool(name="keep", bufs=1))
+        ring = ctx.enter_context(tc.tile_pool(name="ring", bufs=2))
+        acc = ctx.enter_context(tc.psum_pool(name="acc", bufs=4))
+        turn = ctx.enter_context(tc.psum_pool(name="turn", bufs=2))
+
+        def load_scale_rows(queue, plane, rows, quadrants):
+            for q in quadrants:
+                queue.dma_start(plane[32 * q : 32 * q + 4, :].bitcast(I32), rows[0, 4 * q : 4 * q + 4, :].bitcast(I32))
+
+        offs_sb = keep.tile([P, S // 16], U16, name="offs_sb")
+        s1_sb = keep.tile([P, U // 16], U16, name="s1_sb")
+        s2_sb = keep.tile([P, U // 16], U16, name="s2_sb")
+        x_table = keep.tile([P, T], I32, name="x_table", align_bytes=64)
+        x_plane = keep.tile([P, T], U8, name="x_plane", align_bytes=64)
+        w_raw = [keep.tile([P, 2 * H], U8, name="w_raw%d" % i, align_bytes=64) for i in range(2)]
+        w_plane_raw = [keep.tile([P, H], U8, name="w_plane_raw%d" % i, align_bytes=64) for i in range(2)]
+        w_codes = [keep.tile([P, PACK, 2 * P], U8, name="w_codes%d" % i, align_bytes=64) for i in range(3)]
+        w_plane = [keep.tile([P, PACK, P], U8, name="w_plane%d" % i, align_bytes=64) for i in range(3)]
+        unit_sb = keep.tile([P, PACK], F32, name="unit_sb")
+        ident = keep.tile([P, P], F32, name="ident")
+
+        nc.vector.memset(x_plane[:].bitcast(I32), 0)
+        for i in (1, 0):
+            nc.gpsimd.memset(w_plane_raw[i][:].bitcast(I32), 0)
+
+        nc.scalar.dma_start(x_table[:], x_words[0].rearrange("p n t -> p (n t)").bitcast(I32))
+        nc.sync.dma_start(offs_sb[:], offs)
+        load_scale_rows(nc.sync, x_plane, x_scales, range(4))
+        nc.sync.dma_start(w_raw[0][:].bitcast(I32), w1_words[0].bitcast(I32))
+        nc.sync.dma_start(w_raw[1][:].bitcast(I32), w2_words[0].bitcast(I32))
+        load_scale_rows(nc.sync, w_plane_raw[0], w1_scales, range(4))
+        load_scale_rows(nc.gpsimd, w_plane_raw[1], w2_scales, range(2))
+        load_scale_rows(nc.sync, w_plane_raw[1], w2_scales, range(2, 4))
+        nc.sync.dma_start(s2_sb[:], s2)
+        nc.sync.dma_start(s1_sb[:], s1)
+        nc.gpsimd.dma_start(unit_sb[:], unit.rearrange("(p t) o -> p (t o)", t=PACK))
+        make_identity(nc, ident[:])
+
+        def deal(i, raw, tiles):
+            nc.vector.tensor_copy(
+                w_codes[i][:, tiles, :].rearrange("p t (m b) -> p t m b", b=2),
+                w_raw[raw][:].rearrange("p (m t b) -> p t m b", t=PACK, b=2)[:, tiles],
+            )
+            nc.vector.tensor_copy(w_plane[i][:, tiles, :], w_plane_raw[raw][:].rearrange("p (m t) -> p t m", t=PACK)[:, tiles])
+
+        picked_plane = keep.tile([P, S], U8, name="picked_plane", align_bytes=64)
+        nc.vector.tensor_copy(picked_plane[:], x_plane[:].indirect(offs_sb[:]))
+        deal(0, 0, slice(0, 1))
+        picked = keep.tile([P, S], U32, name="picked", align_bytes=64)
+        nc.vector.tensor_copy(picked[:], x_table[:].bitcast(U32).indirect(offs_sb[:]))
+        deal(1, 1, slice(0, 1))
+        deal(0, 0, slice(1, PACK))
+        deal(1, 1, slice(1, PACK))
+        nc.sync.dma_start(w_raw[0][:].bitcast(I32), w3_words[0].bitcast(I32))
+        load_scale_rows(nc.sync, w_plane_raw[0], w3_scales, range(4))
+
+        def product(out, i, t, codes, plane):
+            nc.tensor.matmul_mx(
+                out,
+                lhsT=w_codes[i][:, t, :].bitcast(FP4X4),
+                lhsT_scale=w_plane[i][:, t, :],
+                rhs=codes.bitcast(FP8X4),
+                rhs_scale=plane,
+                start=True,
+                stop=True,
+            )
+
+        y_rows = [keep.tile([P, S], F32, name="y_rows%d" % t) for t in range(PACK)]
+        minus_z = [keep.tile([P, S], F32, name="minus_z%d" % t) for t in range(PACK)]
+        minus_uy = [keep.tile([P, S], F32, name="minus_uy%d" % t) for t in range(PACK)]
+        for t in range(PACK):
+            y_bank = acc.tile([P, S], F32, name="bank")
+            product(y_bank[:], 0, t, picked[:], picked_plane[:])
+            z_bank = acc.tile([P, S], F32, name="bank")
+            product(z_bank[:], 1, t, picked[:], picked_plane[:])
+            if t == 0:
+                nc.scalar.copy(y_rows[t][:], y_bank[:])
+            else:
+                nc.vector.tensor_copy(y_rows[t][:], y_bank[:])
+            nc.vector.tensor_scalar(minus_z[t][:], z_bank[:], -1.0, None, ALU.mult)
+        for t in range(PACK):
+            nc.vector.tensor_scalar(minus_uy[t][:], y_rows[t][:], unit_sb[:, t : t + 1], -1.0, ALU.mult, ALU.mult)
+        deal(2, 0, slice(0, PACK))
+
+        out_codes = keep.tile([P, U], I32, name="out_codes", align_bytes=64)
+        out_plane = keep.tile([P, U], U8, name="out_plane", align_bytes=64)
+        out_rows = out_0.rearrange("(p t) r -> p t r", t=PACK)
+        out_words = out_1[0].rearrange("p n t -> p (n t)").bitcast(I32)
+
+        stages = [(c, h) for c in range(U // CHUNK) for h in range(PACK // PAIR)]
+        st = {}
+
+        def lists(c):
+            cols = slice(c * CHUNK // 16, (c + 1) * CHUNK // 16)
+            return s1_sb[:, cols], s2_sb[:, cols]
+
+        def fetch_difference(s, j):
+            c, h = stages[s]
+            t = PAIR * h + j
+            first, second = lists(c)
+            if j == 0:
+                st["turned", s] = turn.tile([P, PAIR * CHUNK], F32, name="turned")
+            z1 = ring.tile([P, CHUNK], F32, name="z1", bufs=4)
+            y2 = ring.tile([P, CHUNK], F32, name="y2", bufs=4)
+            nc.scalar.activation(y2[:], y_rows[t][:].indirect(second), ACT.Copy)
+            nc.scalar.activation(z1[:], minus_z[t][:].indirect(first), ACT.Copy)
+            for b in range(CHUNK // P):
+                dst = st["turned", s][:, j * CHUNK + b * P : j * CHUNK + (b + 1) * P]
+                nc.tensor.matmul(dst, y2[:, b * P : (b + 1) * P], ident[:], start=True, stop=False, is_transpose=True)
+                nc.tensor.matmul(dst, z1[:, b * P : (b + 1) * P], ident[:], start=False, stop=True, is_transpose=True)
+
+        def magnitude(s):
+            mag = ring.tile([P, PAIR * CHUNK], F32, name="mag")
+            nc.scalar.activation(mag[:], st["turned", s][:], ACT.Abs)
+            back = turn.tile([P, PAIR * CHUNK], F32, name="back")
+            for b in range(PAIR * CHUNK // P):
+                nc.tensor.transpose(back[:, b * P : (b + 1) * P], mag[:, b * P : (b + 1) * P], ident[:])
+            st["back", s] = back
+
+        def inverse_root(s):
+            root = ring.tile([P, PAIR * CHUNK], F32, name="root", bufs=3)
+            nc.scalar.activation(root[:], st["back", s][:], ACT.Abs_reciprocal_sqrt, bias=0.8)
+            st["root", s] = root
+
+        def factors(s):
+            c, h = stages[s]
+            first, second = lists(c)
+            if h == 0:
+                st["left", c] = ring.tile([P, PACK, CHUNK], F32, name="left")
+                st["right", c] = ring.tile([P, PACK, CHUNK], F32, name="right")
+            for j in range(PAIR):
+                t = PAIR * h + j
+                root = st["root", s][:, j * CHUNK : (j + 1) * CHUNK]
+                nc.vector.tensor_tensor(st["left", c][:, t, :], minus_uy[t][:].indirect(first), root, ALU.mult)
+                nc.vector.tensor_tensor(st["right", c][:, t, :], minus_z[t][:].indirect(second), root, ALU.mult)
+
+        def hidden(c):
+            hid = ring.tile([P, CHUNK, PACK], BF16, name="hid", align_bytes=64)
+            nc.vector.tensor_tensor(
+                hid[:].rearrange("p (g i) t -> p g t i", i=4),
+                st["left", c][:].rearrange("p t (g i) -> p g t i", i=4),
+                st["right", c][:].rearrange("p t (g i) -> p g t i", i=4),
+                ALU.mult,
+            )
+            st["hid", c] = hid
+
+        def last_product(c):
+            codes = ring.tile([P, CHUNK], U32, name="hid_codes", align_bytes=64)
+            plane = ring.tile([P, CHUNK], U8, name="hid_plane", align_bytes=64)
+            nc.vector.quantize_mx(codes[:].bitcast(FP8X4), plane[:], st["hid", c][:].rearrange("p n t -> p (n t)"))
+            banks = []
+            for h in range(PACK // PAIR):
+                bank = acc.tile([P, PAIR * CHUNK], F32, name="bank")
+                for j in range(PAIR):
+                    product(bank[:, j * CHUNK : (j + 1) * CHUNK], 2, PAIR * h + j, codes[:], plane[:])
+                banks.append(bank)
+            st["banks", c] = banks
+
+        def result(c):
+            res = ring.tile([P, PACK, CHUNK], F32, name="res")
+            for h in range(PACK // PAIR):
+                nc.scalar.copy(res[:, PAIR * h : PAIR * (h + 1), :].rearrange("p t n -> p (t n)"), st["banks", c][h][:])
+            nc.sync.dma_start(out_rows[:, :, c * CHUNK : (c + 1) * CHUNK], res[:])
+            st["res", c] = res
+
+        def round_result(c):
+            rounded = ring.tile([P, CHUNK, PACK], BF16, name="rounded", align_bytes=64)
+            nc.vector.tensor_copy(
+                rounded[:].rearrange("p (g i) t -> p g t i", i=4), st["res", c][:].rearrange("p t (g i) -> p g t i", i=4)
+            )
+            st["rounded", c] = rounded
+
+        def planes(c):
+            cols = slice(c * CHUNK, (c + 1) * CHUNK)
+            nc.vector.quantize_mx(out_codes[:, cols].bitcast(FP8X4), out_plane[:, cols], st["rounded", c][:].rearrange("p n t -> p (n t)"))
+            nc.sync.dma_start(out_words[:, cols], out_codes[:, cols])
+
+        n_stages = len(stages)
+        for s in range(n_stages + 4):
+            if s < n_stages:
+                fetch_difference(s, 0)
+            if 0 <= s - 1 < n_stages:
+                magnitude(s - 1)
+            if s < n_stages:
+                fetch_difference(s, 1)
+            if 0 <= s - 1 < n_stages:
+                inverse_root(s - 1)
+            if s % 2 == 1 and s >= 3 and (s - 3) // 2 < U // CHUNK:
+                last_product((s - 3) // 2)
+            if s % 2 == 1 and s >= 5:
+                round_result((s - 5) // 2)
+            if 0 <= s - 1 < n_stages:
+                factors(s - 1)
+            if s % 2 == 1 and s >= 5:
+                planes((s - 5) // 2)
+            if s % 2 == 0 and s >= 2 and (s - 2) // 2 < U // CHUNK:
+                hidden((s - 2) // 2)
+            if s % 2 == 0 and s >= 4:
+                result((s - 4) // 2)
+        for q in range(4):
+            nc.sync.dma_start(out_2[0, 4 * q : 4 * q + 4, :].bitcast(I32), out_plane[32 * q : 32 * q + 4, :].bitcast(I32))

@@ -19,8 +19,9 @@ ALU = mybir.AluOpType
 
 P = 128
 PACK = 4
-CHUNK = 256
-PAIR = 2
+BANK = 512
+SPARE = 16
+CHUNKS = [(512, 1), (384, 1), (128, 2)]
 
 
 def tile_picked_yfusgat_rel_po_kernel(
@@ -52,35 +53,42 @@ def tile_picked_yfusgat_rel_po_kernel(
         nc.vector.memset(x_plane[:].bitcast(I32), 0)
         for i in (1, 0):
             nc.gpsimd.memset(w_plane_raw[i][:].bitcast(I32), 0)
+        warm = keep.tile([P, 2], F32, name="warm")
+        nc.vector.memset(warm[:, 0:1], 1.0)
+        nc.scalar.activation(warm[:, 1:2], warm[:, 0:1], ACT.Abs_reciprocal_sqrt)
 
-        nc.scalar.dma_start(x_table[:], x_words[0].rearrange("p n t -> p (n t)").bitcast(I32))
-        nc.sync.dma_start(offs_sb[:], offs)
+        x_rows = x_words[0].rearrange("p n t -> p (n t)").bitcast(I32)
+        nc.sync.dma_start(x_table[:, : T // 2], x_rows[:, : T // 2])
         load_scale_rows(nc.sync, x_plane, x_scales, range(4))
+        nc.sync.dma_start(offs_sb[:], offs)
         nc.sync.dma_start(w_raw[0][:].bitcast(I32), w1_words[0].bitcast(I32))
-        nc.sync.dma_start(w_raw[1][:].bitcast(I32), w2_words[0].bitcast(I32))
+        nc.sync.dma_start(x_table[:, T // 2 :], x_rows[:, T // 2 :])
         load_scale_rows(nc.sync, w_plane_raw[0], w1_scales, range(4))
+        nc.sync.dma_start(w_raw[1][:].bitcast(I32), w2_words[0].bitcast(I32))
         load_scale_rows(nc.gpsimd, w_plane_raw[1], w2_scales, range(2))
         load_scale_rows(nc.sync, w_plane_raw[1], w2_scales, range(2, 4))
         nc.sync.dma_start(s2_sb[:], s2)
         nc.sync.dma_start(s1_sb[:], s1)
-        nc.gpsimd.dma_start(unit_sb[:], unit.rearrange("(p t) o -> p (t o)", t=PACK))
+        nc.sync.dma_start(unit_sb[:], unit.rearrange("(p t) o -> p (t o)", t=PACK))
         make_identity(nc, ident[:])
 
-        def deal(i, raw, tiles):
+        def deal_words(i, raw):
             nc.vector.tensor_copy(
-                w_codes[i][:, tiles, :].rearrange("p t (m b) -> p t m b", b=2),
-                w_raw[raw][:].rearrange("p (m t b) -> p t m b", t=PACK, b=2)[:, tiles],
+                w_codes[i][:].rearrange("p t (m b) -> p t m b", b=2),
+                w_raw[raw][:].rearrange("p (m t b) -> p t m b", t=PACK, b=2),
             )
-            nc.vector.tensor_copy(w_plane[i][:, tiles, :], w_plane_raw[raw][:].rearrange("p (m t) -> p t m", t=PACK)[:, tiles])
 
+        def deal_plane(i, raw):
+            nc.vector.tensor_copy(w_plane[i][:], w_plane_raw[raw][:].rearrange("p (m t) -> p t m", t=PACK))
+
+        deal_words(0, 0)
         picked_plane = keep.tile([P, S], U8, name="picked_plane", align_bytes=64)
         nc.vector.tensor_copy(picked_plane[:], x_plane[:].indirect(offs_sb[:]))
-        deal(0, 0, slice(0, 1))
         picked = keep.tile([P, S], U32, name="picked", align_bytes=64)
         nc.vector.tensor_copy(picked[:], x_table[:].bitcast(U32).indirect(offs_sb[:]))
-        deal(1, 1, slice(0, 1))
-        deal(0, 0, slice(1, PACK))
-        deal(1, 1, slice(1, PACK))
+        deal_plane(0, 0)
+        deal_words(1, 1)
+        deal_plane(1, 1)
         nc.sync.dma_start(w_raw[0][:].bitcast(I32), w3_words[0].bitcast(I32))
         load_scale_rows(nc.sync, w_plane_raw[0], w3_scales, range(4))
 
@@ -95,77 +103,75 @@ def tile_picked_yfusgat_rel_po_kernel(
                 stop=True,
             )
 
-        y_rows = [keep.tile([P, S], F32, name="y_rows%d" % t) for t in range(PACK)]
-        minus_z = [keep.tile([P, S], F32, name="minus_z%d" % t) for t in range(PACK)]
-        minus_uy = [keep.tile([P, S], F32, name="minus_uy%d" % t) for t in range(PACK)]
-        for t in range(PACK):
-            y_bank = acc.tile([P, S], F32, name="bank")
-            product(y_bank[:], 0, t, picked[:], picked_plane[:])
-            z_bank = acc.tile([P, S], F32, name="bank")
-            product(z_bank[:], 1, t, picked[:], picked_plane[:])
-            if t == 0:
-                nc.scalar.copy(y_rows[t][:], y_bank[:])
-            else:
-                nc.vector.tensor_copy(y_rows[t][:], y_bank[:])
-            nc.vector.tensor_scalar(minus_z[t][:], z_bank[:], -1.0, None, ALU.mult)
-        for t in range(PACK):
-            nc.vector.tensor_scalar(minus_uy[t][:], y_rows[t][:], unit_sb[:, t : t + 1], -1.0, ALU.mult, ALU.mult)
-        deal(2, 0, slice(0, PACK))
+        y_rows = [keep.tile([P, S + SPARE], F32, name="y_rows%d" % t) for t in range(PACK)]
+        minus_z = [keep.tile([P, S + SPARE], F32, name="minus_z%d" % t) for t in range(PACK)]
+        minus_uy = [keep.tile([P, S + SPARE], F32, name="minus_uy%d" % t) for t in range(PACK)]
+        for window in y_rows + minus_z + minus_uy:
+            nc.gpsimd.memset(window[:, S:], 0.0)
 
         out_codes = keep.tile([P, U], I32, name="out_codes", align_bytes=64)
         out_plane = keep.tile([P, U], U8, name="out_plane", align_bytes=64)
         out_rows = out_0.rearrange("(p t) r -> p t r", t=PACK)
         out_words = out_1[0].rearrange("p n t -> p (n t)").bitcast(I32)
 
-        stages = [(c, h) for c in range(U // CHUNK) for h in range(PACK // PAIR)]
+        starts = [sum(width for width, tiles in CHUNKS[:c]) for c in range(len(CHUNKS))]
+        stages = [[(c, t, 0, width) for t in range(first, first + tiles)] for c, (width, tiles) in enumerate(CHUNKS) for first in range(0, PACK, tiles)]
+        last_stage = {piece[0]: s for s, stage in enumerate(stages) for piece in stage}
+        last_chunk = len(CHUNKS) - 1
         st = {}
 
-        def lists(c):
-            cols = slice(c * CHUNK // 16, (c + 1) * CHUNK // 16)
+        def lists(c, lo, n):
+            cols = slice((starts[c] + lo) // 16, (starts[c] + lo + n) // 16)
             return s1_sb[:, cols], s2_sb[:, cols]
 
-        def fetch_difference(s, j):
-            c, h = stages[s]
-            t = PAIR * h + j
-            first, second = lists(c)
-            if j == 0:
-                st["turned", s] = turn.tile([P, PAIR * CHUNK], F32, name="turned")
-            z1 = ring.tile([P, CHUNK], F32, name="z1", bufs=4)
-            y2 = ring.tile([P, CHUNK], F32, name="y2", bufs=4)
-            nc.scalar.activation(y2[:], y_rows[t][:].indirect(second), ACT.Copy)
-            nc.scalar.activation(z1[:], minus_z[t][:].indirect(first), ACT.Copy)
-            for b in range(CHUNK // P):
-                dst = st["turned", s][:, j * CHUNK + b * P : j * CHUNK + (b + 1) * P]
-                nc.tensor.matmul(dst, y2[:, b * P : (b + 1) * P], ident[:], start=True, stop=False, is_transpose=True)
-                nc.tensor.matmul(dst, z1[:, b * P : (b + 1) * P], ident[:], start=False, stop=True, is_transpose=True)
+        def fetch_difference(s, half):
+            stage = stages[s]
+            width = len(stage) * stage[0][3]
+            if half == 0:
+                st["turned", s] = turn.tile([P, width], F32, name="turned")
+            term = ring.tile([P, width], F32, name="term", bufs=3)
+            for j, (c, t, lo, n) in enumerate(stage):
+                first, second = lists(c, lo, n)
+                window = y_rows[t][:].indirect(second) if half == 0 else minus_z[t][:].indirect(first)
+                if half == 1 and s < 2:
+                    nc.vector.tensor_copy(term[:, j * n : (j + 1) * n], window)
+                else:
+                    nc.scalar.activation(term[:, j * n : (j + 1) * n], window, ACT.Copy)
+            blocks = width // P
+            for b in range(blocks):
+                cols = slice(b * P, (b + 1) * P)
+                nc.tensor.matmul(
+                    st["turned", s][:, cols], term[:, cols], ident[:],
+                    start=(half == 0 and b == 0), stop=(half == 1 and b == blocks - 1), is_transpose=True,
+                )
 
         def magnitude(s):
-            mag = ring.tile([P, PAIR * CHUNK], F32, name="mag")
+            width = len(stages[s]) * stages[s][0][3]
+            mag = ring.tile([P, width], F32, name="mag")
             nc.scalar.activation(mag[:], st["turned", s][:], ACT.Abs)
-            back = turn.tile([P, PAIR * CHUNK], F32, name="back")
-            for b in range(PAIR * CHUNK // P):
+            back = turn.tile([P, width], F32, name="back")
+            for b in range(width // P):
                 nc.tensor.transpose(back[:, b * P : (b + 1) * P], mag[:, b * P : (b + 1) * P], ident[:])
             st["back", s] = back
 
         def inverse_root(s):
-            root = ring.tile([P, PAIR * CHUNK], F32, name="root", bufs=3)
+            width = len(stages[s]) * stages[s][0][3]
+            root = ring.tile([P, width], F32, name="root", bufs=3)
             nc.scalar.activation(root[:], st["back", s][:], ACT.Abs_reciprocal_sqrt, bias=0.8)
             st["root", s] = root
 
         def factors(s):
-            c, h = stages[s]
-            first, second = lists(c)
-            if h == 0:
-                st["left", c] = ring.tile([P, PACK, CHUNK], F32, name="left")
-                st["right", c] = ring.tile([P, PACK, CHUNK], F32, name="right")
-            for j in range(PAIR):
-                t = PAIR * h + j
-                root = st["root", s][:, j * CHUNK : (j + 1) * CHUNK]
-                nc.vector.tensor_tensor(st["left", c][:, t, :], minus_uy[t][:].indirect(first), root, ALU.mult)
-                nc.vector.tensor_tensor(st["right", c][:, t, :], minus_z[t][:].indirect(second), root, ALU.mult)
+            for j, (c, t, lo, n) in enumerate(stages[s]):
+                first, second = lists(c, lo, n)
+                if t == 0 and lo == 0:
+                    st["left", c] = ring.tile([P, PACK, CHUNKS[c][0]], F32, name="left")
+                    st["right", c] = ring.tile([P, PACK, CHUNKS[c][0]], F32, name="right")
+                root = st["root", s][:, j * n : (j + 1) * n]
+                nc.vector.tensor_tensor(st["left", c][:, t, lo : lo + n], minus_uy[t][:].indirect(first), root, ALU.mult)
+                nc.vector.tensor_tensor(st["right", c][:, t, lo : lo + n], minus_z[t][:].indirect(second), root, ALU.mult)
 
         def hidden(c):
-            hid = ring.tile([P, CHUNK, PACK], BF16, name="hid", align_bytes=64)
+            hid = ring.tile([P, CHUNKS[c][0], PACK], BF16, name="hid", align_bytes=64)
             nc.vector.tensor_tensor(
                 hid[:].rearrange("p (g i) t -> p g t i", i=4),
                 st["left", c][:].rearrange("p t (g i) -> p g t i", i=4),
@@ -175,57 +181,98 @@ def tile_picked_yfusgat_rel_po_kernel(
             st["hid", c] = hid
 
         def last_product(c):
-            codes = ring.tile([P, CHUNK], U32, name="hid_codes", align_bytes=64)
-            plane = ring.tile([P, CHUNK], U8, name="hid_plane", align_bytes=64)
+            n = CHUNKS[c][0]
+            codes = ring.tile([P, n], U32, name="hid_codes", align_bytes=64)
+            plane = ring.tile([P, n], U8, name="hid_plane", align_bytes=64)
             nc.vector.quantize_mx(codes[:].bitcast(FP8X4), plane[:], st["hid", c][:].rearrange("p n t -> p (n t)"))
             banks = []
-            for h in range(PACK // PAIR):
-                bank = acc.tile([P, PAIR * CHUNK], F32, name="bank")
-                for j in range(PAIR):
-                    product(bank[:, j * CHUNK : (j + 1) * CHUNK], 2, PAIR * h + j, codes[:], plane[:])
-                banks.append(bank)
+            per_bank = BANK // n
+            for t in range(PACK):
+                j = t % per_bank
+                if j == 0:
+                    banks.append(acc.tile([P, per_bank * n], F32, name="bank"))
+                for lo, hi in ([(0, 256), (256, n)] if n == 384 else [(0, n)]):
+                    product(banks[-1][:, j * n + lo : j * n + hi], 2, t, codes[:, lo:hi], plane[:, lo:hi])
             st["banks", c] = banks
 
         def result(c):
-            res = ring.tile([P, PACK, CHUNK], F32, name="res")
-            for h in range(PACK // PAIR):
-                nc.scalar.copy(res[:, PAIR * h : PAIR * (h + 1), :].rearrange("p t n -> p (t n)"), st["banks", c][h][:])
-            nc.sync.dma_start(out_rows[:, :, c * CHUNK : (c + 1) * CHUNK], res[:])
+            n = CHUNKS[c][0]
+            res = ring.tile([P, PACK * n], F32, name="res")
+            for b, bank in enumerate(st["banks", c]):
+                width = bank.shape[1]
+                nc.scalar.copy(res[:, b * width : (b + 1) * width], bank[:])
+            nc.sync.dma_start(out_rows[:, :, starts[c] : starts[c] + n], res[:].rearrange("p (t n) -> p t n", t=PACK))
             st["res", c] = res
 
-        def round_result(c):
-            rounded = ring.tile([P, CHUNK, PACK], BF16, name="rounded", align_bytes=64)
-            nc.vector.tensor_copy(
-                rounded[:].rearrange("p (g i) t -> p g t i", i=4), st["res", c][:].rearrange("p t (g i) -> p g t i", i=4)
+        def round_result(c, source):
+            rounded = ring.tile([P, CHUNKS[c][0], PACK], BF16, name="rounded", align_bytes=64)
+            (nc.scalar.copy if c < last_chunk else nc.vector.tensor_copy)(
+                rounded[:].rearrange("p (g i) t -> p g t i", i=4), source[:].rearrange("p (t g i) -> p g t i", t=PACK, i=4)
             )
             st["rounded", c] = rounded
 
         def planes(c):
-            cols = slice(c * CHUNK, (c + 1) * CHUNK)
+            cols = slice(starts[c], starts[c] + CHUNKS[c][0])
             nc.vector.quantize_mx(out_codes[:, cols].bitcast(FP8X4), out_plane[:, cols], st["rounded", c][:].rearrange("p n t -> p (n t)"))
             nc.sync.dma_start(out_words[:, cols], out_codes[:, cols])
 
-        n_stages = len(stages)
-        for s in range(n_stages + 4):
-            if s < n_stages:
+        def chunks_ending(s):
+            return [c for c in last_stage if last_stage[c] == s]
+
+        def scalar_step(s):
+            if s < len(stages):
                 fetch_difference(s, 0)
-            if 0 <= s - 1 < n_stages:
+            if s - 1 < len(stages):
                 magnitude(s - 1)
-            if s < n_stages:
+            if s < len(stages):
                 fetch_difference(s, 1)
-            if 0 <= s - 1 < n_stages:
+            if s - 1 < len(stages):
                 inverse_root(s - 1)
-            if s % 2 == 1 and s >= 3 and (s - 3) // 2 < U // CHUNK:
-                last_product((s - 3) // 2)
-            if s % 2 == 1 and s >= 5:
-                round_result((s - 5) // 2)
+
+        def y_product(t, copy):
+            bank = acc.tile([P, S], F32, name="bank")
+            product(bank[:], 0, t, picked[:], picked_plane[:])
+            copy(y_rows[t][:, :S], bank[:])
+
+        def z_product(t):
+            bank = acc.tile([P, S], F32, name="bank")
+            product(bank[:], 1, t, picked[:], picked_plane[:])
+            nc.vector.tensor_scalar(minus_z[t][:, :S], bank[:], -1.0, None, ALU.mult)
+
+        y_product(0, nc.scalar.copy)
+        y_product(1, nc.scalar.copy)
+        z_product(0)
+        fetch_difference(0, 0)
+        fetch_difference(0, 1)
+        z_product(1)
+        scalar_step(1)
+        for t in range(2, PACK):
+            y_product(t, nc.vector.tensor_copy)
+            z_product(t)
+        for t in range(PACK):
+            nc.gpsimd.tensor_scalar(minus_uy[t][:, :S], y_rows[t][:, :S], unit_sb[:, t : t + 1], -1.0, ALU.mult, ALU.mult)
+        deal_words(2, 0)
+        deal_plane(2, 0)
+
+        n_stages = len(stages)
+        for s in range(1, n_stages + 4):
+            if s > 1:
+                scalar_step(s)
+            for c in chunks_ending(s - 2):
+                last_product(c)
+            for c in chunks_ending(s - 4):
+                if c != last_chunk:
+                    round_result(c, st["res", c])
             if 0 <= s - 1 < n_stages:
                 factors(s - 1)
-            if s % 2 == 1 and s >= 5:
-                planes((s - 5) // 2)
-            if s % 2 == 0 and s >= 2 and (s - 2) // 2 < U // CHUNK:
-                hidden((s - 2) // 2)
-            if s % 2 == 0 and s >= 4:
-                result((s - 4) // 2)
+            for c in chunks_ending(s - 4):
+                planes(c)
+            for c in chunks_ending(s - 1):
+                hidden(c)
+            for c in chunks_ending(s - 3):
+                if c == last_chunk:
+                    round_result(c, st["banks", c][0])
+                result(c)
         for q in range(4):
-            nc.sync.dma_start(out_2[0, 4 * q : 4 * q + 4, :].bitcast(I32), out_plane[32 * q : 32 * q + 4, :].bitcast(I32))
+            queue = nc.sync if q % 2 == 0 else nc.scalar
+            queue.dma_start(out_2[0, 4 * q : 4 * q + 4, :].bitcast(I32), out_plane[32 * q : 32 * q + 4, :].bitcast(I32))

@@ -21,7 +21,7 @@ P = 128
 PACK = 4
 BANK = 512
 SPARE = 16
-CHUNKS = [(512, 1), (384, 1), (128, 2)]
+CHUNKS = [(512, [1, 1, 1, 1]), (384, [1, 1, 1, 1]), (128, [3, 1])]
 
 
 def tile_picked_yfusgat_rel_po_kernel(
@@ -43,7 +43,7 @@ def tile_picked_yfusgat_rel_po_kernel(
         s2_sb = keep.tile([P, U // 16], U16, name="s2_sb")
         x_table = keep.tile([P, T], I32, name="x_table", align_bytes=64)
         x_plane = keep.tile([P, T], U8, name="x_plane", align_bytes=64)
-        w_raw = [keep.tile([P, 2 * H], U8, name="w_raw%d" % i, align_bytes=64) for i in range(2)]
+        w_raw = [keep.tile([P, 2 * H], U8, name="w_raw%d" % i, align_bytes=64) for i in range(3)]
         w_plane_raw = [keep.tile([P, H], U8, name="w_plane_raw%d" % i, align_bytes=64) for i in range(2)]
         w_codes = [keep.tile([P, PACK, 2 * P], U8, name="w_codes%d" % i, align_bytes=64) for i in range(3)]
         w_plane = [keep.tile([P, PACK, P], U8, name="w_plane%d" % i, align_bytes=64) for i in range(3)]
@@ -58,15 +58,16 @@ def tile_picked_yfusgat_rel_po_kernel(
         nc.scalar.activation(warm[:, 1:2], warm[:, 0:1], ACT.Abs_reciprocal_sqrt)
 
         x_rows = x_words[0].rearrange("p n t -> p (n t)").bitcast(I32)
-        nc.sync.dma_start(x_table[:, : T // 2], x_rows[:, : T // 2])
+        nc.sync.dma_start(x_table[:, : T // 4], x_rows[:, : T // 4])
         load_scale_rows(nc.sync, x_plane, x_scales, range(4))
         nc.sync.dma_start(offs_sb[:], offs)
         nc.sync.dma_start(w_raw[0][:].bitcast(I32), w1_words[0].bitcast(I32))
-        nc.sync.dma_start(x_table[:, T // 2 :], x_rows[:, T // 2 :])
+        nc.sync.dma_start(x_table[:, T // 4 :], x_rows[:, T // 4 :])
         load_scale_rows(nc.sync, w_plane_raw[0], w1_scales, range(4))
         nc.sync.dma_start(w_raw[1][:].bitcast(I32), w2_words[0].bitcast(I32))
-        load_scale_rows(nc.gpsimd, w_plane_raw[1], w2_scales, range(2))
-        load_scale_rows(nc.sync, w_plane_raw[1], w2_scales, range(2, 4))
+        load_scale_rows(nc.gpsimd, w_plane_raw[1], w2_scales, range(3))
+        load_scale_rows(nc.sync, w_plane_raw[1], w2_scales, range(3, 4))
+        nc.sync.dma_start(w_raw[2][:].bitcast(I32), w3_words[0].bitcast(I32))
         nc.sync.dma_start(s2_sb[:], s2)
         nc.sync.dma_start(s1_sb[:], s1)
         nc.sync.dma_start(unit_sb[:], unit.rearrange("(p t) o -> p (t o)", t=PACK))
@@ -89,7 +90,7 @@ def tile_picked_yfusgat_rel_po_kernel(
         deal_plane(0, 0)
         deal_words(1, 1)
         deal_plane(1, 1)
-        nc.sync.dma_start(w_raw[0][:].bitcast(I32), w3_words[0].bitcast(I32))
+        deal_words(2, 2)
         load_scale_rows(nc.sync, w_plane_raw[0], w3_scales, range(4))
 
         def product(out, i, t, codes, plane):
@@ -115,7 +116,7 @@ def tile_picked_yfusgat_rel_po_kernel(
         out_words = out_1[0].rearrange("p n t -> p (n t)").bitcast(I32)
 
         starts = [sum(width for width, tiles in CHUNKS[:c]) for c in range(len(CHUNKS))]
-        stages = [[(c, t, 0, width) for t in range(first, first + tiles)] for c, (width, tiles) in enumerate(CHUNKS) for first in range(0, PACK, tiles)]
+        stages = [[(c, t, 0, width) for t in range(sum(tiles[:k]), sum(tiles[: k + 1]))] for c, (width, tiles) in enumerate(CHUNKS) for k in range(len(tiles))]
         last_stage = {piece[0]: s for s, stage in enumerate(stages) for piece in stage}
         last_chunk = len(CHUNKS) - 1
         st = {}
@@ -133,7 +134,7 @@ def tile_picked_yfusgat_rel_po_kernel(
             for j, (c, t, lo, n) in enumerate(stage):
                 first, second = lists(c, lo, n)
                 window = y_rows[t][:].indirect(second) if half == 0 else minus_z[t][:].indirect(first)
-                if half == 1 and s < 2:
+                if half == 1 and s < 3:
                     nc.vector.tensor_copy(term[:, j * n : (j + 1) * n], window)
                 else:
                     nc.scalar.activation(term[:, j * n : (j + 1) * n], window, ACT.Copy)
@@ -245,13 +246,13 @@ def tile_picked_yfusgat_rel_po_kernel(
         fetch_difference(0, 0)
         fetch_difference(0, 1)
         z_product(1)
+        y_product(2, nc.scalar.copy)
         scalar_step(1)
-        for t in range(2, PACK):
-            y_product(t, nc.vector.tensor_copy)
-            z_product(t)
+        z_product(2)
+        y_product(3, nc.vector.tensor_copy)
+        z_product(3)
         for t in range(PACK):
             nc.gpsimd.tensor_scalar(minus_uy[t][:, :S], y_rows[t][:, :S], unit_sb[:, t : t + 1], -1.0, ALU.mult, ALU.mult)
-        deal_words(2, 0)
         deal_plane(2, 0)
 
         n_stages = len(stages)

from contextlib import ExitStack

import concourse.mybir as mybir
from concourse.masks import make_identity

K, T, S, H, U = 512, 2048, 512, 512, 1024
FLOPS = 2 * K * H * S * 2 + 2 * H * H * U

F32 = mybir.dt.float32
BF16 = mybir.dt.bfloat16
I32 = mybir.dt.int32
U32 = mybir.dt.uint32
U16 = mybir.dt.uint16
U8 = mybir.dt.uint8
FP8X4 = mybir.dt.float8_e4m3fn_x4
FP4X4 = mybir.dt.float4_e2m1fn_x4
ACT = mybir.ActivationFunctionType
ALU = mybir.AluOpType

P = 128
PACK = 4
BANK = 512
SPARE = 16
CHUNKS = [(512, [1, 1, 1, 1]), (384, [1, 1, 1, 1]), (128, [3, 1])]


def tile_picked_yfusgat_rel_po_kernel(
    tc, x_words, x_scales, w1_words, w1_scales, w2_words, w2_scales, unit, w3_words, w3_scales, offs, s1, s2, out_0, out_1, out_2
):
    nc = tc.nc
    with ExitStack() as ctx:
        keep = ctx.enter_context(tc.tile_pool(name="keep", bufs=1))
        ring = ctx.enter_context(tc.tile_pool(name="ring", bufs=2))
        acc = ctx.enter_context(tc.psum_pool(name="acc", bufs=4))
        turn = ctx.enter_context(tc.psum_pool(name="turn", bufs=2))

        def load_scale_rows(queue, plane, rows, quadrants):
            for q in quadrants:
                queue.dma_start(plane[32 * q : 32 * q + 4, :].bitcast(I32), rows[0, 4 * q : 4 * q + 4, :].bitcast(I32))

        offs_sb = keep.tile([P, S // 16], U16, name="offs_sb")
        s1_sb = keep.tile([P, U // 16], U16, name="s1_sb")
        s2_sb = keep.tile([P, U // 16], U16, name="s2_sb")
        x_table = keep.tile([P, T], I32, name="x_table", align_bytes=64)
        x_plane = keep.tile([P, T], U8, name="x_plane", align_bytes=64)
        w_raw = [keep.tile([P, 2 * H], U8, name="w_raw%d" % i, align_bytes=64) for i in range(3)]
        w_plane_raw = [keep.tile([P, H], U8, name="w_plane_raw%d" % i, align_bytes=64) for i in range(2)]
        w_codes = [keep.tile([P, PACK, 2 * P], U8, name="w_codes%d" % i, align_bytes=64) for i in range(3)]
        w_plane = [keep.tile([P, PACK, P], U8, name="w_plane%d" % i, align_bytes=64) for i in range(3)]
        unit_sb = keep.tile([P, PACK], F32, name="unit_sb")
        ident = keep.tile([P, P], F32, name="ident")

        nc.vector.memset(x_plane[:].bitcast(I32), 0)
        for i in (1, 0):
            nc.gpsimd.memset(w_plane_raw[i][:].bitcast(I32), 0)
        warm = keep.tile([P, 2], F32, name="warm")
        nc.vector.memset(warm[:, 0:1], 1.0)
        nc.scalar.activation(warm[:, 1:2], warm[:, 0:1], ACT.Abs_reciprocal_sqrt)

        x_rows = x_words[0].rearrange("p n t -> p (n t)").bitcast(I32)
        nc.sync.dma_start(x_table[:, : T // 4], x_rows[:, : T // 4])
        load_scale_rows(nc.sync, x_plane, x_scales, range(4))
        nc.sync.dma_start(offs_sb[:], offs)
        nc.sync.dma_start(w_raw[0][:].bitcast(I32), w1_words[0].bitcast(I32))
        nc.sync.dma_start(x_table[:, T // 4 :], x_rows[:, T // 4 :])
        load_scale_rows(nc.sync, w_plane_raw[0], w1_scales, range(4))
        nc.sync.dma_start(w_raw[1][:].bitcast(I32), w2_words[0].bitcast(I32))
        load_scale_rows(nc.gpsimd, w_plane_raw[1], w2_scales, range(3))
        load_scale_rows(nc.sync, w_plane_raw[1], w2_scales, range(3, 4))
        nc.sync.dma_start(w_raw[2][:].bitcast(I32), w3_words[0].bitcast(I32))
        nc.sync.dma_start(s2_sb[:], s2)
        nc.sync.dma_start(s1_sb[:], s1)
        nc.sync.dma_start(unit_sb[:], unit.rearrange("(p t) o -> p (t o)", t=PACK))
        make_identity(nc, ident[:])

        def deal_words(i, raw):
            nc.vector.tensor_copy(
                w_codes[i][:].rearrange("p t (m b) -> p t m b", b=2),
                w_raw[raw][:].rearrange("p (m t b) -> p t m b", t=PACK, b=2),
            )

        def deal_plane(i, raw):
            nc.vector.tensor_copy(w_plane[i][:], w_plane_raw[raw][:].rearrange("p (m t) -> p t m", t=PACK))

        deal_words(0, 0)
        picked_plane = keep.tile([P, S], U8, name="picked_plane", align_bytes=64)
        nc.vector.tensor_copy(picked_plane[:], x_plane[:].indirect(offs_sb[:]))
        picked = keep.tile([P, S], U32, name="picked", align_bytes=64)
        nc.vector.tensor_copy(picked[:], x_table[:].bitcast(U32).indirect(offs_sb[:]))
        deal_plane(0, 0)
        deal_words(1, 1)
        deal_plane(1, 1)
        deal_words(2, 2)
        load_scale_rows(nc.sync, w_plane_raw[0], w3_scales, range(4))

        def product(out, i, t, codes, plane):
            nc.tensor.matmul_mx(
                out,
                lhsT=w_codes[i][:, t, :].bitcast(FP4X4),
                lhsT_scale=w_plane[i][:, t, :],
                rhs=codes.bitcast(FP8X4),
                rhs_scale=plane,
                start=True,
                stop=True,
            )

        y_rows = [keep.tile([P, S + SPARE], F32, name="y_rows%d" % t) for t in range(PACK)]
        minus_z = [keep.tile([P, S + SPARE], F32, name="minus_z%d" % t) for t in range(PACK)]
        minus_uy = [keep.tile([P, S + SPARE], F32, name="minus_uy%d" % t) for t in range(PACK)]
        for window in y_rows + minus_z + minus_uy:
            nc.gpsimd.memset(window[:, S:], 0.0)

        out_codes = keep.tile([P, U], I32, name="out_codes", align_bytes=64)
        out_plane = keep.tile([P, U], U8, name="out_plane", align_bytes=64)
        out_rows = out_0.rearrange("(p t) r -> p t r", t=PACK)
        out_words = out_1[0].rearrange("p n t -> p (n t)").bitcast(I32)

        starts = [sum(width for width, tiles in CHUNKS[:c]) for c in range(len(CHUNKS))]
        stages = [[(c, t, 0, width) for t in range(sum(tiles[:k]), sum(tiles[: k + 1]))] for c, (width, tiles) in enumerate(CHUNKS) for k in range(len(tiles))]
        last_stage = {piece[0]: s for s, stage in enumerate(stages) for piece in stage}
        last_chunk = len(CHUNKS) - 1
        st = {}

        def lists(c, lo, n):
            cols = slice((starts[c] + lo) // 16, (starts[c] + lo + n) // 16)
            return s1_sb[:, cols], s2_sb[:, cols]

        def fetch_difference(s, half):
            stage = stages[s]
            width = len(stage) * stage[0][3]
            if half == 0:
                st["turned", s] = turn.tile([P, width], F32, name="turned")
            term = ring.tile([P, width], F32, name="term", bufs=3)
            for j, (c, t, lo, n) in enumerate(stage):
                first, second = lists(c, lo, n)
                window = y_rows[t][:].indirect(second) if half == 0 else minus_z[t][:].indirect(first)
                if half == 1 and s < 3:
                    nc.vector.tensor_copy(term[:, j * n : (j + 1) * n], window)
                else:
                    nc.scalar.activation(term[:, j * n : (j + 1) * n], window, ACT.Copy)
            blocks = width // P
            for b in range(blocks):
                cols = slice(b * P, (b + 1) * P)
                nc.tensor.matmul(
                    st["turned", s][:, cols], term[:, cols], ident[:],
                    start=(half == 0 and b == 0), stop=(half == 1 and b == blocks - 1), is_transpose=True,
                )

        def magnitude(s):
            width = len(stages[s]) * stages[s][0][3]
            mag = ring.tile([P, width], F32, name="mag")
            nc.scalar.activation(mag[:], st["turned", s][:], ACT.Abs)
            back = turn.tile([P, width], F32, name="back")
            for b in range(width // P):
                nc.tensor.transpose(back[:, b * P : (b + 1) * P], mag[:, b * P : (b + 1) * P], ident[:])
            st["back", s] = back

        def inverse_root(s):
            width = len(stages[s]) * stages[s][0][3]
            root = ring.tile([P, width], F32, name="root", bufs=3)
            nc.scalar.activation(root[:], st["back", s][:], ACT.Abs_reciprocal_sqrt, bias=0.8)
            st["root", s] = root

        def factors(s):
            for j, (c, t, lo, n) in enumerate(stages[s]):
                first, second = lists(c, lo, n)
                if t == 0 and lo == 0:
                    st["left", c] = ring.tile([P, PACK, CHUNKS[c][0]], F32, name="left")
                    st["right", c] = ring.tile([P, PACK, CHUNKS[c][0]], F32, name="right")
                root = st["root", s][:, j * n : (j + 1) * n]
                nc.vector.tensor_tensor(st["left", c][:, t, lo : lo + n], minus_uy[t][:].indirect(first), root, ALU.mult)
                nc.vector.tensor_tensor(st["right", c][:, t, lo : lo + n], minus_z[t][:].indirect(second), root, ALU.mult)

        def hidden(c):
            hid = ring.tile([P, CHUNKS[c][0], PACK], BF16, name="hid", align_bytes=64)
            nc.vector.tensor_tensor(
                hid[:].rearrange("p (g i) t -> p g t i", i=4),
                st["left", c][:].rearrange("p t (g i) -> p g t i", i=4),
                st["right", c][:].rearrange("p t (g i) -> p g t i", i=4),
                ALU.mult,
            )
            st["hid", c] = hid

        def last_product(c):
            n = CHUNKS[c][0]
            codes = ring.tile([P, n], U32, name="hid_codes", align_bytes=64)
            plane = ring.tile([P, n], U8, name="hid_plane", align_bytes=64)
            nc.vector.quantize_mx(codes[:].bitcast(FP8X4), plane[:], st["hid", c][:].rearrange("p n t -> p (n t)"))
            banks = []
            per_bank = BANK // n
            for t in range(PACK):
                j = t % per_bank
                if j == 0:
                    banks.append(acc.tile([P, per_bank * n], F32, name="bank"))
                for lo, hi in ([(0, 256), (256, n)] if n == 384 else [(0, n)]):
                    product(banks[-1][:, j * n + lo : j * n + hi], 2, t, codes[:, lo:hi], plane[:, lo:hi])
            st["banks", c] = banks

        def result(c):
            n = CHUNKS[c][0]
            res = ring.tile([P, PACK * n], F32, name="res")
            for b, bank in enumerate(st["banks", c]):
                width = bank.shape[1]
                nc.scalar.copy(res[:, b * width : (b + 1) * width], bank[:])
            nc.sync.dma_start(out_rows[:, :, starts[c] : starts[c] + n], res[:].rearrange("p (t n) -> p t n", t=PACK))
            st["res", c] = res

        def round_result(c, source):
            rounded = ring.tile([P, CHUNKS[c][0], PACK], BF16, name="rounded", align_bytes=64)
            (nc.scalar.copy if c < last_chunk else nc.vector.tensor_copy)(
                rounded[:].rearrange("p (g i) t -> p g t i", i=4), source[:].rearrange("p (t g i) -> p g t i", t=PACK, i=4)
            )
            st["rounded", c] = rounded

        def planes(c):
            cols = slice(starts[c], starts[c] + CHUNKS[c][0])
            nc.vector.quantize_mx(out_codes[:, cols].bitcast(FP8X4), out_plane[:, cols], st["rounded", c][:].rearrange("p n t -> p (n t)"))
            nc.sync.dma_start(out_words[:, cols], out_codes[:, cols])

        def chunks_ending(s):
            return [c for c in last_stage if last_stage[c] == s]

        def scalar_step(s):
            if s < len(stages):
                fetch_difference(s, 0)
            if s - 1 < len(stages):
                magnitude(s - 1)
            if s < len(stages):
                fetch_difference(s, 1)
            if s - 1 < len(stages):
                inverse_root(s - 1)

        def y_product(t, copy):
            bank = acc.tile([P, S], F32, name="bank")
            product(bank[:], 0, t, picked[:], picked_plane[:])
            copy(y_rows[t][:, :S], bank[:])

        def z_product(t):
            bank = acc.tile([P, S], F32, name="bank")
            product(bank[:], 1, t, picked[:], picked_plane[:])
            nc.vector.tensor_scalar(minus_z[t][:, :S], bank[:], -1.0, None, ALU.mult)

        y_product(0, nc.scalar.copy)
        y_product(1, nc.scalar.copy)
        z_product(0)
        fetch_difference(0, 0)
        fetch_difference(0, 1)
        z_product(1)
        y_product(2, nc.scalar.copy)
        scalar_step(1)
        z_product(2)
        y_product(3, nc.vector.tensor_copy)
        z_product(3)
        for t in range(PACK):
            nc.gpsimd.tensor_scalar(minus_uy[t][:, :S], y_rows[t][:, :S], unit_sb[:, t : t + 1], -1.0, ALU.mult, ALU.mult)
        deal_plane(2, 0)

        n_stages = len(stages)
        for s in range(1, n_stages + 4):
            if s > 1:
                scalar_step(s)
            for c in chunks_ending(s - 2):
                last_product(c)
            for c in chunks_ending(s - 4):
                if c != last_chunk:
                    round_result(c, st["res", c])
            if 0 <= s - 1 < n_stages:
                factors(s - 1)
            for c in chunks_ending(s - 4):
                planes(c)
            for c in chunks_ending(s - 1):
                hidden(c)
            for c in chunks_ending(s - 3):
                if c == last_chunk:
                    round_result(c, st["banks", c][0])
                result(c)
        for q in range(4):
            queue = nc.sync if q % 2 == 0 else nc.scalar
            queue.dma_start(out_2[0, 4 * q : 4 * q + 4, :].bitcast(I32), out_plane[32 * q : 32 * q + 4, :].bitcast(I32))
